import numpy as np, ml_dtypes
CORES = [16,32,48,64,80]
N = 5
import mx_ref
NC = 256
BF = ml_dtypes.bfloat16
def cut(t, i, w=512):
    return t[:, w * i:w * i + w]
def term(a, B):
    return np.stack([np.maximum(mx_ref.matmul(mx_ref.quantize(cut(a, i)), B), 0) for i in range(4)], axis=2).reshape(128, -1)
def setup_inputs(rng):
    def f(*shape):
        return mx_ref.flush((rng.standard_normal(shape, dtype=np.float32) * np.exp2(rng.integers(-2, 3, shape[:-1] + (1,)))).astype(BF))
    return {"a": f(N, 128, 4 * 512), "b": f(N, 128, 4 * NC)}
def setup_inputs_blocks(rng):
    d = setup_inputs(rng)
    for k in ("a", "b"): d[k] = mx_ref.spread(d[k], rng, 2)
    return d
def setup_inputs_wide(rng):
    d = setup_inputs(rng)
    for k in ("a", "b"): d[k] = mx_ref.flush((d[k].astype(np.float32) * np.exp2(rng.integers(-4, 5, (N, 1, 1))).astype(np.float32)).astype(BF))
    return d
def setup_inputs_lossless(rng):
    a = np.zeros((N, 128, 4 * 128, 4), np.float32)
    for r in range(N):
        k = rng.integers(0, 512, size=4 * 128)
        a[r, k // 4, np.arange(4 * 128), k % 4] = 1.0
    size = np.repeat(2.0 ** rng.integers(-4, 5, size=(1, 1, (4 * NC) // 4)), 4, axis=2)
    b = (rng.random((N, 128, 4 * NC)) < 0.8) * size
    return {"a": a.reshape(N, 128, 4 * 512).astype(BF), "b": b.astype(np.float32).astype(BF)}
def reference(a, b):
    Bq = [mx_ref.quantize(b[c]) for c in range(N)]
    y = np.zeros((N, 128, 4 * NC), np.float32)
    for c in range(N):
        y[c] = mx_ref.total([term(a[r], Bq[c]) for r in range(N)])
    return {"y": y}

@@ -1,0 +1,157 @@
+from concourse.bass import DstId, RemoteDMATransfer
+from concourse.mybir import dt, AluOpType, ActivationFunctionType
+
+N = 5
+NC = 256
+NW = 512
+HALF = NW // 2
+SIM_CORES = 96
+BANK = 512
+BANKS = 8
+
+SCRATCH = {
+    "at": ("sbuf", [128, 4 * NW], "bfloat16"),
+    "bt": ("sbuf", [128, 4 * NC], "bfloat16"),
+    "ac": ("sbuf", [128, NW], "float8_e4m3fn_x4"),
+    "ap": ("sbuf", [128, NW], "uint8"),
+    "bc": ("sbuf", [128, NC], "float8_e4m3fn_x4"),
+    "bp": ("sbuf", [128, NC], "uint8"),
+    "yt": ("sbuf", [128, 4 * NC], "float32"),
+    "ps": ("psum", [128, BANK * BANKS], "float32"),
+}
+for _k in range(1, N):
+    SCRATCH["lc%d" % _k] = ("sbuf", [128, NW], "float8_e4m3fn_x4")
+    SCRATCH["lp%d" % _k] = ("sbuf", [128, NW], "uint8")
+for _k in range(N):
+    SCRATCH["h%d" % _k] = ("sbuf", [128, 4 * NC], "bfloat16")
+for _k in range(1, N - 1):
+    SCRATCH["s%d" % _k] = ("sbuf", [128, 4 * NC], "bfloat16")
+SEMAPHORES = (["la0", "la1", "lb", "qa0", "qa1", "qb", "sent", "cin", "pin", "mm", "act", "add", "st0", "st1"]
+              + ["arr%d" % k for k in range(1, N)])
+
+ORDER = [0, 1, 3, 2, 4]
+
+
+def helpers(core, topo):
+    out = []
+    for k in range(SIM_CORES):
+        if topo.chip(k) == topo.chip(core) and topo.die(k) != topo.die(core):
+            if all(topo.addr(k)[2] != topo.addr(o)[2] for o in out):
+                out.append(k)
+    return out[:2]
+
+
+def rank_program(g, core, T, topo):
+    S = T.sem
+    sent = [0]
+
+    def codes(name, a, b):
+        return T[name][:, a:b].bitcast(dt.uint8)
+
+    def copy(dst, out, in_, sem):
+        m = topo.mask(core, dst)
+        rid, pid, _ = topo.addr(dst)
+        g.remote_dma(out, in_, sem, S.sent, pid, rid, m)
+        sent[0] += m.bit_count()
+        return m.bit_count()
+
+    rank = T.rank_of(core)
+    if rank is None:
+        for r in range(N):
+            hs = helpers(T.cores[r], topo)
+            if core in hs:
+                helper_program(g, core, T, topo, r, hs.index(core), codes, copy, sent)
+        return
+
+    hs = helpers(core, topo)
+    g.sync.dma_start(T.at[:, 0:4 * HALF], T.a[:, 0:4 * HALF]).then_inc(S.la0, 16)
+    g.scalar.dma_start(T.at[:, 4 * HALF:4 * NW], T.a[:, 4 * HALF:4 * NW]).then_inc(S.la1, 16)
+    g.sync.dma_start(T.bt[:], T.b[:]).then_inc(S.lb, 16)
+
+    g.vector.wait_ge(S.la0, 16)
+    g.vector.quantize_mx(T.ac[:, 0:HALF], T.ap[:, 0:HALF], T.at[:, 0:4 * HALF]).then_inc(S.qa0, 1)
+    g.vector.wait_ge(S.la1, 16)
+    g.vector.quantize_mx(T.ac[:, HALF:NW], T.ap[:, HALF:NW], T.at[:, 4 * HALF:4 * NW]).then_inc(S.qa1, 1)
+    g.vector.wait_ge(S.lb, 16)
+    g.vector.quantize_mx(T.bc[:], T.bp[:], T.bt[:]).then_inc(S.qb, 1)
+
+    g.wait_ge(S.qa0, 1)
+    copy(hs[0], codes("ac", 0, HALF), codes("ac", 0, HALF), S.cin)
+    g.wait_ge(S.qa1, 1)
+    copy(hs[1], codes("ac", HALF, NW), codes("ac", HALF, NW), S.cin)
+    m = topo.mask(core, hs[0]) & topo.mask(core, hs[1])
+    ids = [DstId(rid=topo.addr(h)[0], pnc=topo.addr(h)[1]) for h in hs]
+    g.remote_dma_fused([RemoteDMATransfer(dst_ids=ids, dma_engine_mask=m, remote_sem=S.pin,
+                                          srcs=[T.ap[:, 0:NW]], dsts=[T.ap[:, 0:NW] for h in hs])], local_sem=S.sent)
+    sent[0] += m.bit_count()
+    for k in (1, 2):
+        dst = T.cores[(rank + k) % N]
+        copy(dst, codes("lc%d" % k, 0, NW), codes("ac", 0, NW), S["arr%d" % k])
+        copy(dst, T["lp%d" % k][:, 0:NW], T.ap[:, 0:NW], S["arr%d" % k])
+    g.wait_ge(S.sent, sent[0])
+
+    items = [(s, i, 0, NC) for s in range(N - 1) for i in range(4)]
+    items += [(N - 1, i, NC // 2 * j, NC // 2) for j in range(2) for i in range(4)]
+
+    def arrivals(k):
+        src = T.cores[(rank - k) % N]
+        eng = topo.mask(src, core).bit_count()
+        return eng * (2 if k in (1, 2) else 3)
+
+    last = None
+    for n, (s, i, j, w) in enumerate(items):
+        k = ORDER[s]
+        if s != last:
+            last = s
+            if k == 0:
+                g.tensor.wait_ge(S.qa0, 1)
+                g.tensor.wait_ge(S.qa1, 1)
+                g.tensor.wait_ge(S.qb, 1)
+            else:
+                g.tensor.wait_ge(S["arr%d" % k], arrivals(k))
+        wc, wp = ("ac", "ap") if k == 0 else ("lc%d" % k, "lp%d" % k)
+        if n >= BANKS:
+            g.tensor.wait_ge(S.act, n - BANKS + 1)
+        bank = BANK * (n % BANKS)
+        g.tensor.matmul_mx(T.ps[:, bank:bank + w], T[wc][:, 128 * i:128 * i + 128], T[wp][:, 128 * i:128 * i + 128],
+                           T.bc[:, j:j + w], T.bp[:, j:j + w], True, True).then_inc(S.mm, 1)
+        g.scalar.wait_ge(S.mm, n + 1)
+        g.scalar.activation(T["h%d" % s][:, 4 * j + i:4 * (j + w):4], T.ps[:, bank:bank + w],
+                            ActivationFunctionType.Relu).then_inc(S.act, 1)
+
+    acc, nadd = "h0", 0
+    for s in range(1, N - 1):
+        g.vector.wait_ge(S.act, 4 * (s + 1))
+        if nadd:
+            g.vector.wait_ge(S.add, nadd)
+        g.vector.tensor_tensor(T["s%d" % s][:], T[acc][:], T["h%d" % s][:], AluOpType.add).then_inc(S.add, 1)
+        acc, nadd = "s%d" % s, nadd + 1
+    for j in range(2):
+        a, b = 2 * NC * j, 2 * NC * (j + 1)
+        g.vector.wait_ge(S.act, 4 * (N - 1) + 4 * (j + 1))
+        g.vector.wait_ge(S.add, nadd)
+        g.vector.tensor_tensor(T.yt[:, a:b], T[acc][:, a:b], T["h%d" % (N - 1)][:, a:b], AluOpType.add).then_inc(S.add, 1)
+        nadd += 1
+        g.sync.wait_ge(S.add, nadd)
+        g.sync.dma_start(T.y[:, a:b], T.yt[:, a:b]).then_inc(S["st%d" % j], 16)
+    g.sync.wait_ge(S.st0, 16)
+    g.sync.wait_ge(S.st1, 16)
+
+
+def helper_program(g, core, T, topo, r, part, codes, copy, sent):
+    S = T.sem
+    eng = topo.mask(T.cores[r], core).bit_count()
+    a, b = HALF * part, HALF * (part + 1)
+
+    def plane(k):
+        g.wait_ge(S.pin, eng)
+        copy(T.cores[(r + k) % N], T["lp%d" % k][:, 0:NW], T.ap[:, 0:NW], S["arr%d" % k])
+
+    g.wait_ge(S.cin, eng)
+    copy(T.cores[(r + 3) % N], codes("lc3", a, b), codes("ac", a, b), S.arr3)
+    if part == 0:
+        plane(3)
+    copy(T.cores[(r + 4) % N], codes("lc4", a, b), codes("ac", a, b), S.arr4)
+    if part == 1:
+        plane(4)
+    g.wait_ge(S.sent, sent[0])

@@ -1,10 +1,10 @@
-from concourse.bass import DstId, RemoteDMATransfer
 from concourse.mybir import dt, AluOpType, ActivationFunctionType
 
 N = 5
 NC = 256
 NW = 512
-HALF = NW // 2
+TILE = 128
+HEAD = TILE
 SIM_CORES = 96
 BANK = 512
 BANKS = 8
@@ -16,6 +16,7 @@ SCRATCH = {
     "ap": ("sbuf", [128, NW], "uint8"),
     "bc": ("sbuf", [128, NC], "float8_e4m3fn_x4"),
     "bp": ("sbuf", [128, NC], "uint8"),
+    "yb": ("sbuf", [128, 4 * NC], "bfloat16"),
     "yt": ("sbuf", [128, 4 * NC], "float32"),
     "ps": ("psum", [128, BANK * BANKS], "float32"),
 }
@@ -26,10 +27,14 @@ for _k in range(N):
     SCRATCH["h%d" % _k] = ("sbuf", [128, 4 * NC], "bfloat16")
 for _k in range(1, N - 1):
     SCRATCH["s%d" % _k] = ("sbuf", [128, 4 * NC], "bfloat16")
-SEMAPHORES = (["la0", "la1", "lb", "qa0", "qa1", "qb", "sent", "cin", "pin", "mm", "act", "add", "st0", "st1"]
-              + ["arr%d" % k for k in range(1, N)])
+SEMAPHORES = (["la0", "la1", "lb", "qa0", "qa1", "qb", "sent", "cin", "mm", "act", "vr", "add", "wide", "fin0", "fin1",
+               "st0", "st1", "head2", "head3", "head4", "rest3", "rest4"] + ["arr%d" % k for k in range(1, N)])
 
 ORDER = [0, 1, 3, 2, 4]
+ON_VECTOR = [(1, 3), (2, 3)]
+PARTS = [(0, HEAD), (HEAD, NW)]
+PASS_ON = [(3, 2, 4), (3, 4)]
+WIDEN = 320
 
 
 def helpers(core, topo):
@@ -41,117 +46,126 @@ def helpers(core, topo):
     return out[:2]
 
 
+def helper_mask(core, part, h, k, topo):
+    return topo.mask(core, h) if part else topo.mask(core, h) & ~topo.mask(core, k)
+
+
 def rank_program(g, core, T, topo):
     S = T.sem
     sent = [0]
 
-    def codes(name, a, b):
-        return T[name][:, a:b].bitcast(dt.uint8)
-
-    def copy(dst, out, in_, sem):
-        m = topo.mask(core, dst)
+    def copy(dst, out, in_, sem, m=None):
+        if m is None:
+            m = topo.mask(core, dst)
         rid, pid, _ = topo.addr(dst)
         g.remote_dma(out, in_, sem, S.sent, pid, rid, m)
         sent[0] += m.bit_count()
-        return m.bit_count()
+
+    def codes(dst, name, a, b, sem, m=None):
+        copy(dst, T[name][:, a:b].bitcast(dt.uint8), T.ac[:, a:b].bitcast(dt.uint8), sem, m)
 
     rank = T.rank_of(core)
     if rank is None:
         for r in range(N):
-            hs = helpers(T.cores[r], topo)
+            src = T.cores[r]
+            hs = helpers(src, topo)
             if core in hs:
-                helper_program(g, core, T, topo, r, hs.index(core), codes, copy, sent)
+                part = hs.index(core)
+                a, b = PARTS[part]
+                g.wait_ge(S.cin, helper_mask(src, part, core, T.cores[(r + 1) % N], topo).bit_count())
+                for k in PASS_ON[part]:
+                    codes(T.cores[(r + k) % N], "lc%d" % k, a, b, S["%s%d" % ("rest" if part else "head", k)])
+                g.wait_ge(S.sent, sent[0])
         return
 
+    V, A, X = g.vector, g.scalar, g.tensor
     hs = helpers(core, topo)
-    g.sync.dma_start(T.at[:, 0:4 * HALF], T.a[:, 0:4 * HALF]).then_inc(S.la0, 16)
-    g.scalar.dma_start(T.at[:, 4 * HALF:4 * NW], T.a[:, 4 * HALF:4 * NW]).then_inc(S.la1, 16)
+    dests = [T.cores[(rank + k) % N] for k in range(N)]
+
+    g.sync.dma_start(T.at[:, 0:4 * HEAD], T.a[:, 0:4 * HEAD]).then_inc(S.la0, 16)
+    g.sync.dma_start(T.at[:, 4 * HEAD:4 * NW], T.a[:, 4 * HEAD:4 * NW]).then_inc(S.la1, 16)
     g.sync.dma_start(T.bt[:], T.b[:]).then_inc(S.lb, 16)
 
-    g.vector.wait_ge(S.la0, 16)
-    g.vector.quantize_mx(T.ac[:, 0:HALF], T.ap[:, 0:HALF], T.at[:, 0:4 * HALF]).then_inc(S.qa0, 1)
-    g.vector.wait_ge(S.la1, 16)
-    g.vector.quantize_mx(T.ac[:, HALF:NW], T.ap[:, HALF:NW], T.at[:, 4 * HALF:4 * NW]).then_inc(S.qa1, 1)
-    g.vector.wait_ge(S.lb, 16)
-    g.vector.quantize_mx(T.bc[:], T.bp[:], T.bt[:]).then_inc(S.qb, 1)
-
-    g.wait_ge(S.qa0, 1)
-    copy(hs[0], codes("ac", 0, HALF), codes("ac", 0, HALF), S.cin)
-    g.wait_ge(S.qa1, 1)
-    copy(hs[1], codes("ac", HALF, NW), codes("ac", HALF, NW), S.cin)
-    m = topo.mask(core, hs[0]) & topo.mask(core, hs[1])
-    ids = [DstId(rid=topo.addr(h)[0], pnc=topo.addr(h)[1]) for h in hs]
-    g.remote_dma_fused([RemoteDMATransfer(dst_ids=ids, dma_engine_mask=m, remote_sem=S.pin,
-                                          srcs=[T.ap[:, 0:NW]], dsts=[T.ap[:, 0:NW] for h in hs])], local_sem=S.sent)
-    sent[0] += m.bit_count()
-    for k in (1, 2):
-        dst = T.cores[(rank + k) % N]
-        copy(dst, codes("lc%d" % k, 0, NW), codes("ac", 0, NW), S["arr%d" % k])
-        copy(dst, T["lp%d" % k][:, 0:NW], T.ap[:, 0:NW], S["arr%d" % k])
+    for part, (a, b) in enumerate(PARTS):
+        V.wait_ge(S["la%d" % part], 16)
+        V.quantize_mx(T.ac[:, a:b], T.ap[:, a:b], T.at[:, 4 * a:4 * b]).then_inc(S["qa%d" % part], 1)
+        g.wait_ge(S["qa%d" % part], 1)
+        codes(hs[part], "ac", a, b, S.cin, helper_mask(core, part, hs[part], dests[1], topo))
+    V.wait_ge(S.lb, 16)
+    V.quantize_mx(T.bc[:], T.bp[:], T.bt[:]).then_inc(S.qb, 1)
+    for k in (1, 3, 2, 4):
+        if k in (1, 2):
+            codes(dests[k], "lc%d" % k, 0 if k == 1 else HEAD, NW, S["arr%d" % k])
+        copy(dests[k], T["lp%d" % k][:, 0:NW], T.ap[:, 0:NW], S["arr%d" % k])
     g.wait_ge(S.sent, sent[0])
 
-    items = [(s, i, 0, NC) for s in range(N - 1) for i in range(4)]
-    items += [(N - 1, i, NC // 2 * j, NC // 2) for j in range(2) for i in range(4)]
+    last = N - 1
+    items = [(s, i, 0, NC) for s in range(last) for i in range(4)]
+    items += [(last, i, NC // 2 * j, NC // 2) for j in range(2) for i in range(4)]
+    n = {"act": 0, "vr": 0}
+    free = {}
+    waited = set()
 
-    def arrivals(k):
-        src = T.cores[(rank - k) % N]
-        eng = topo.mask(src, core).bit_count()
-        return eng * (2 if k in (1, 2) else 3)
+    def ready(k, i):
+        if k == 0:
+            need = [("qa0", 1), ("qa1", 1), ("qb", 1)]
+        else:
+            eng = topo.mask(T.cores[(rank - k) % N], core).bit_count()
+            need = [("arr%d" % k, 2 * eng if k in (1, 2) else eng)]
+            if k > 1 and TILE * i < HEAD:
+                need.append(("head%d" % k, eng))
+            if k > 2 and TILE * i >= HEAD:
+                need.append(("rest%d" % k, eng))
+        for w in need:
+            if w not in waited:
+                waited.add(w)
+                X.wait_ge(S[w[0]], w[1])
 
-    last = None
-    for n, (s, i, j, w) in enumerate(items):
+    acc, nadd, half = "h0", 0, 0
+    for m, (s, i, j, w) in enumerate(items):
         k = ORDER[s]
-        if s != last:
-            last = s
-            if k == 0:
-                g.tensor.wait_ge(S.qa0, 1)
-                g.tensor.wait_ge(S.qa1, 1)
-                g.tensor.wait_ge(S.qb, 1)
-            else:
-                g.tensor.wait_ge(S["arr%d" % k], arrivals(k))
+        ready(k, i)
+        bank = m % BANKS
+        if bank in free:
+            X.wait_ge(*free[bank])
+        out = T.ps[:, BANK * bank:BANK * bank + w]
         wc, wp = ("ac", "ap") if k == 0 else ("lc%d" % k, "lp%d" % k)
-        if n >= BANKS:
-            g.tensor.wait_ge(S.act, n - BANKS + 1)
-        bank = BANK * (n % BANKS)
-        g.tensor.matmul_mx(T.ps[:, bank:bank + w], T[wc][:, 128 * i:128 * i + 128], T[wp][:, 128 * i:128 * i + 128],
-                           T.bc[:, j:j + w], T.bp[:, j:j + w], True, True).then_inc(S.mm, 1)
-        g.scalar.wait_ge(S.mm, n + 1)
-        g.scalar.activation(T["h%d" % s][:, 4 * j + i:4 * (j + w):4], T.ps[:, bank:bank + w],
-                            ActivationFunctionType.Relu).then_inc(S.act, 1)
-
-    acc, nadd = "h0", 0
-    for s in range(1, N - 1):
-        g.vector.wait_ge(S.act, 4 * (s + 1))
+        c = TILE * i
+        X.matmul_mx(out, T[wc][:, c:c + TILE], T[wp][:, c:c + TILE], T.bc[:, j:j + w], T.bp[:, j:j + w],
+                    True, True).then_inc(S.mm, 1)
+        h = T["h%d" % s][:, 4 * j + i:4 * (j + w):4]
+        if (s, i) in ON_VECTOR:
+            V.wait_ge(S.mm, m + 1)
+            V.tensor_scalar(h, out, 0.0, None, AluOpType.max).then_inc(S.vr, 1)
+            n["vr"] += 1
+            free[bank] = (S.vr, n["vr"])
+        else:
+            A.wait_ge(S.mm, m + 1)
+            A.activation(h, out, ActivationFunctionType.Relu).then_inc(S.act, 1)
+            n["act"] += 1
+            free[bank] = (S.act, n["act"])
+        if i < 3 or s == 0:
+            continue
+        V.wait_ge(S.act, n["act"])
+        if n["vr"]:
+            V.wait_ge(S.vr, n["vr"])
         if nadd:
-            g.vector.wait_ge(S.add, nadd)
-        g.vector.tensor_tensor(T["s%d" % s][:], T[acc][:], T["h%d" % s][:], AluOpType.add).then_inc(S.add, 1)
-        acc, nadd = "s%d" % s, nadd + 1
-    for j in range(2):
-        a, b = 2 * NC * j, 2 * NC * (j + 1)
-        g.vector.wait_ge(S.act, 4 * (N - 1) + 4 * (j + 1))
-        g.vector.wait_ge(S.add, nadd)
-        g.vector.tensor_tensor(T.yt[:, a:b], T[acc][:, a:b], T["h%d" % (N - 1)][:, a:b], AluOpType.add).then_inc(S.add, 1)
-        nadd += 1
-        g.sync.wait_ge(S.add, nadd)
-        g.sync.dma_start(T.y[:, a:b], T.yt[:, a:b]).then_inc(S["st%d" % j], 16)
+            V.wait_ge(S.add, nadd)
+        if s < last:
+            V.tensor_tensor(T["s%d" % s][:], T[acc][:], T["h%d" % s][:], AluOpType.add).then_inc(S.add, 1)
+            acc, nadd = "s%d" % s, nadd + 1
+        else:
+            a, b, e = 4 * j, 4 * j + WIDEN, 4 * (j + w)
+            V.tensor_tensor(T.yb[:, a:b], T[acc][:, a:b], T["h%d" % s][:, a:b], AluOpType.add).then_inc(S.wide, 1)
+            V.tensor_tensor(T.yt[:, b:e], T[acc][:, b:e], T["h%d" % s][:, b:e], AluOpType.add).then_inc(S["fin%d" % half], 1)
+            half += 1
+
+    for half in range(2):
+        a, b = 2 * NC * half, 2 * NC * (half + 1)
+        A.wait_ge(S.wide, half + 1)
+        A.activation(T.yt[:, a:a + WIDEN], T.yb[:, a:a + WIDEN],
+                     ActivationFunctionType.Copy).then_inc(S["fin%d" % half], 1)
+        g.sync.wait_ge(S["fin%d" % half], 2)
+        g.sync.dma_start(T.y[:, a:b], T.yt[:, a:b]).then_inc(S["st%d" % half], 16)
     g.sync.wait_ge(S.st0, 16)
     g.sync.wait_ge(S.st1, 16)
-
-
-def helper_program(g, core, T, topo, r, part, codes, copy, sent):
-    S = T.sem
-    eng = topo.mask(T.cores[r], core).bit_count()
-    a, b = HALF * part, HALF * (part + 1)
-
-    def plane(k):
-        g.wait_ge(S.pin, eng)
-        copy(T.cores[(r + k) % N], T["lp%d" % k][:, 0:NW], T.ap[:, 0:NW], S["arr%d" % k])
-
-    g.wait_ge(S.cin, eng)
-    copy(T.cores[(r + 3) % N], codes("lc3", a, b), codes("ac", a, b), S.arr3)
-    if part == 0:
-        plane(3)
-    copy(T.cores[(r + 4) % N], codes("lc4", a, b), codes("ac", a, b), S.arr4)
-    if part == 1:
-        plane(4)
-    g.wait_ge(S.sent, sent[0])

from concourse.mybir import dt, AluOpType, ActivationFunctionType

N = 5
NC = 256
NW = 512
TILE = 128
HEAD = TILE
SIM_CORES = 96
BANK = 512
BANKS = 8

SCRATCH = {
    "at": ("sbuf", [128, 4 * NW], "bfloat16"),
    "bt": ("sbuf", [128, 4 * NC], "bfloat16"),
    "ac": ("sbuf", [128, NW], "float8_e4m3fn_x4"),
    "ap": ("sbuf", [128, NW], "uint8"),
    "bc": ("sbuf", [128, NC], "float8_e4m3fn_x4"),
    "bp": ("sbuf", [128, NC], "uint8"),
    "yb": ("sbuf", [128, 4 * NC], "bfloat16"),
    "yt": ("sbuf", [128, 4 * NC], "float32"),
    "ps": ("psum", [128, BANK * BANKS], "float32"),
}
for _k in range(1, N):
    SCRATCH["lc%d" % _k] = ("sbuf", [128, NW], "float8_e4m3fn_x4")
    SCRATCH["lp%d" % _k] = ("sbuf", [128, NW], "uint8")
for _k in range(N):
    SCRATCH["h%d" % _k] = ("sbuf", [128, 4 * NC], "bfloat16")
for _k in range(1, N - 1):
    SCRATCH["s%d" % _k] = ("sbuf", [128, 4 * NC], "bfloat16")
SEMAPHORES = (["la0", "la1", "lb", "qa0", "qa1", "qb", "sent", "cin", "mm", "act", "vr", "add", "wide", "fin0", "fin1",
               "st0", "st1", "head2", "head3", "head4", "rest3", "rest4"] + ["arr%d" % k for k in range(1, N)])

ORDER = [0, 1, 3, 2, 4]
ON_VECTOR = [(1, 3), (2, 3)]
PARTS = [(0, HEAD), (HEAD, NW)]
PASS_ON = [(3, 2, 4), (3, 4)]
WIDEN = 320


def helpers(core, topo):
    out = []
    for k in range(SIM_CORES):
        if topo.chip(k) == topo.chip(core) and topo.die(k) != topo.die(core):
            if all(topo.addr(k)[2] != topo.addr(o)[2] for o in out):
                out.append(k)
    return out[:2]


def helper_mask(core, part, h, k, topo):
    return topo.mask(core, h) if part else topo.mask(core, h) & ~topo.mask(core, k)


def rank_program(g, core, T, topo):
    S = T.sem
    sent = [0]

    def copy(dst, out, in_, sem, m=None):
        if m is None:
            m = topo.mask(core, dst)
        rid, pid, _ = topo.addr(dst)
        g.remote_dma(out, in_, sem, S.sent, pid, rid, m)
        sent[0] += m.bit_count()

    def codes(dst, name, a, b, sem, m=None):
        copy(dst, T[name][:, a:b].bitcast(dt.uint8), T.ac[:, a:b].bitcast(dt.uint8), sem, m)

    rank = T.rank_of(core)
    if rank is None:
        for r in range(N):
            src = T.cores[r]
            hs = helpers(src, topo)
            if core in hs:
                part = hs.index(core)
                a, b = PARTS[part]
                g.wait_ge(S.cin, helper_mask(src, part, core, T.cores[(r + 1) % N], topo).bit_count())
                for k in PASS_ON[part]:
                    codes(T.cores[(r + k) % N], "lc%d" % k, a, b, S["%s%d" % ("rest" if part else "head", k)])
                g.wait_ge(S.sent, sent[0])
        return

    V, A, X = g.vector, g.scalar, g.tensor
    hs = helpers(core, topo)
    dests = [T.cores[(rank + k) % N] for k in range(N)]

    g.sync.dma_start(T.at[:, 0:4 * HEAD], T.a[:, 0:4 * HEAD]).then_inc(S.la0, 16)
    g.sync.dma_start(T.at[:, 4 * HEAD:4 * NW], T.a[:, 4 * HEAD:4 * NW]).then_inc(S.la1, 16)
    g.sync.dma_start(T.bt[:], T.b[:]).then_inc(S.lb, 16)

    for part, (a, b) in enumerate(PARTS):
        V.wait_ge(S["la%d" % part], 16)
        V.quantize_mx(T.ac[:, a:b], T.ap[:, a:b], T.at[:, 4 * a:4 * b]).then_inc(S["qa%d" % part], 1)
        g.wait_ge(S["qa%d" % part], 1)
        codes(hs[part], "ac", a, b, S.cin, helper_mask(core, part, hs[part], dests[1], topo))
    V.wait_ge(S.lb, 16)
    V.quantize_mx(T.bc[:], T.bp[:], T.bt[:]).then_inc(S.qb, 1)
    for k in (1, 3, 2, 4):
        if k in (1, 2):
            codes(dests[k], "lc%d" % k, 0 if k == 1 else HEAD, NW, S["arr%d" % k])
        copy(dests[k], T["lp%d" % k][:, 0:NW], T.ap[:, 0:NW], S["arr%d" % k])
    g.wait_ge(S.sent, sent[0])

    last = N - 1
    items = [(s, i, 0, NC) for s in range(last) for i in range(4)]
    items += [(last, i, NC // 2 * j, NC // 2) for j in range(2) for i in range(4)]
    n = {"act": 0, "vr": 0}
    free = {}
    waited = set()

    def ready(k, i):
        if k == 0:
            need = [("qa0", 1), ("qa1", 1), ("qb", 1)]
        else:
            eng = topo.mask(T.cores[(rank - k) % N], core).bit_count()
            need = [("arr%d" % k, 2 * eng if k in (1, 2) else eng)]
            if k > 1 and TILE * i < HEAD:
                need.append(("head%d" % k, eng))
            if k > 2 and TILE * i >= HEAD:
                need.append(("rest%d" % k, eng))
        for w in need:
            if w not in waited:
                waited.add(w)
                X.wait_ge(S[w[0]], w[1])

    acc, nadd, half = "h0", 0, 0
    for m, (s, i, j, w) in enumerate(items):
        k = ORDER[s]
        ready(k, i)
        bank = m % BANKS
        if bank in free:
            X.wait_ge(*free[bank])
        out = T.ps[:, BANK * bank:BANK * bank + w]
        wc, wp = ("ac", "ap") if k == 0 else ("lc%d" % k, "lp%d" % k)
        c = TILE * i
        X.matmul_mx(out, T[wc][:, c:c + TILE], T[wp][:, c:c + TILE], T.bc[:, j:j + w], T.bp[:, j:j + w],
                    True, True).then_inc(S.mm, 1)
        h = T["h%d" % s][:, 4 * j + i:4 * (j + w):4]
        if (s, i) in ON_VECTOR:
            V.wait_ge(S.mm, m + 1)
            V.tensor_scalar(h, out, 0.0, None, AluOpType.max).then_inc(S.vr, 1)
            n["vr"] += 1
            free[bank] = (S.vr, n["vr"])
        else:
            A.wait_ge(S.mm, m + 1)
            A.activation(h, out, ActivationFunctionType.Relu).then_inc(S.act, 1)
            n["act"] += 1
            free[bank] = (S.act, n["act"])
        if i < 3 or s == 0:
            continue
        V.wait_ge(S.act, n["act"])
        if n["vr"]:
            V.wait_ge(S.vr, n["vr"])
        if nadd:
            V.wait_ge(S.add, nadd)
        if s < last:
            V.tensor_tensor(T["s%d" % s][:], T[acc][:], T["h%d" % s][:], AluOpType.add).then_inc(S.add, 1)
            acc, nadd = "s%d" % s, nadd + 1
        else:
            a, b, e = 4 * j, 4 * j + WIDEN, 4 * (j + w)
            V.tensor_tensor(T.yb[:, a:b], T[acc][:, a:b], T["h%d" % s][:, a:b], AluOpType.add).then_inc(S.wide, 1)
            V.tensor_tensor(T.yt[:, b:e], T[acc][:, b:e], T["h%d" % s][:, b:e], AluOpType.add).then_inc(S["fin%d" % half], 1)
            half += 1

    for half in range(2):
        a, b = 2 * NC * half, 2 * NC * (half + 1)
        A.wait_ge(S.wide, half + 1)
        A.activation(T.yt[:, a:a + WIDEN], T.yb[:, a:a + WIDEN],
                     ActivationFunctionType.Copy).then_inc(S["fin%d" % half], 1)
        g.sync.wait_ge(S["fin%d" % half], 2)
        g.sync.dma_start(T.y[:, a:b], T.yt[:, a:b]).then_inc(S["st%d" % half], 16)
    g.sync.wait_ge(S.st0, 16)
    g.sync.wait_ge(S.st1, 16)
